import numpy as np
import ml_dtypes


def mxq(x, axis, fmt="e4m3"):
    dtype, down = {"e4m3": (ml_dtypes.float8_e4m3fn, 7), "e5m2": (ml_dtypes.float8_e5m2, 14)}[fmt]
    v = np.moveaxis(np.asarray(x, np.float32).astype(ml_dtypes.bfloat16).astype(np.float64), axis, -1)
    blocks = v.reshape(v.shape[:-1] + (-1, 32))
    amax = np.abs(blocks).max(-1, keepdims=True)
    byte = np.maximum(np.where(amax > 0, np.frexp(amax)[1] - 1 + 127, 0) - down, 1)
    scale = np.exp2(byte - 127.0)
    codes = (blocks / scale).astype(np.float32).astype(dtype).astype(np.float64)
    return np.moveaxis((codes * scale).reshape(v.shape), -1, axis)


WIDE = False


def mx_kscale(k):
    if not WIDE:
        return np.ones(k)
    levels = np.array([10, -10, 5, -5, 0])
    if k % 512:
        return np.exp2(np.random.permutation(np.resize(levels, k // 32))).repeat(32)
    a = np.empty((k // 512, 16))
    for p in range(k // 512):
        a[p, :8] = np.random.permutation(np.resize(levels, 8))
        for g in range(8):
            far = levels[np.abs(levels - a[p, g]) >= 10]
            a[p, g + 8] = far[np.random.randint(len(far))]
    return np.exp2(a.ravel()).repeat(32)


BF16 = ml_dtypes.bfloat16


def bf(x):
    return np.asarray(x, np.float32).astype(BF16)


def f64(x):
    return np.asarray(x).astype(np.float64)


E2M1 = np.array([0.0, 0.5, 1.0, 1.5, 2.0, 3.0, 4.0, 6.0, -0.0, -0.5, -1.0, -1.5, -2.0, -3.0, -4.0, -6.0])


def pack_weight(w, fmt):
    k, n = w.shape
    w = f64(bf(w)).reshape(k // 32, 32, n)
    amax = np.abs(w).max(1)
    if fmt == "e4m3":
        byte = np.frexp(amax)[1] - 1 + 127 - 7
    else:
        mant, ex = np.frexp(amax / 6.0)
        byte = np.where(mant > 0.5, ex, ex - 1) + 127
    byte = np.clip(np.where(amax > 0, byte, 1), 1, 254)
    scaled = (w * np.exp2(127.0 - byte)[:, None, :]).reshape(k, n).astype(np.float32)
    by_word = np.ascontiguousarray(scaled.reshape(k // 512, 128, 4, n).transpose(0, 1, 3, 2))
    if fmt == "e4m3":
        words = by_word.astype(ml_dtypes.float8_e4m3fn).view(np.uint8)
    else:
        c = by_word.astype(ml_dtypes.float4_e2m1fn).view(np.uint8) & 0xF
        words = c[..., 0::2] | (c[..., 1::2] << 4)
    return np.ascontiguousarray(words), np.ascontiguousarray(byte.astype(np.uint8).reshape(k // 512, 16, n))


def unpack_weight(words, scales, fmt):
    g, p, n, _ = words.shape
    if fmt == "e4m3":
        vals = np.ascontiguousarray(words).view(ml_dtypes.float8_e4m3fn).astype(np.float64)
    else:
        nib = np.empty((g, p, n, 4), np.uint8)
        nib[..., 0::2] = words & 0xF
        nib[..., 1::2] = words >> 4
        vals = E2M1[nib]
    vals = vals * np.repeat(np.exp2(scales.astype(np.float64) - 127.0), 8, axis=1)[..., None]
    return vals.transpose(0, 1, 3, 2).reshape(g * 512, n)
def pack4(w):
    words, scales = pack_weight(w, "e2m1")
    return words.reshape(words.shape[0], 128, -1), scales


def unpack4(words, scales):
    return unpack_weight(words.reshape(words.shape[0], 128, -1, 2), scales, "e2m1")


def planes(Y):
    n, m = Y.shape
    b = f64(bf(Y)).reshape(n // 32, 32, m)
    amax = np.abs(b).max(1)
    byte = np.clip(np.where(amax > 0, np.frexp(amax)[1] - 1 + 127 - 7, 1), 1, 254)
    codes = (b * np.exp2(127.0 - byte)[:, None, :]).reshape(n, m).astype(np.float32).astype(ml_dtypes.float8_e4m3fn).view(np.uint8)
    words = codes.reshape(n // 512, 128, 4, m).transpose(0, 1, 3, 2)
    return np.ascontiguousarray(words), np.ascontiguousarray(byte.astype(np.uint8).reshape(n // 512, 16, m))


Q, E, F, D = 512, 1536, 2048, 1024


def setup_inputs():
    s = mx_kscale(E)
    t = mx_kscale(F)
    x = np.random.randn(Q, E)
    w1 = np.random.randn(E, F) / np.sqrt(E)
    w2 = 1.5 * np.random.randn(F, D) / np.sqrt(F)
    x_words, x_scales = pack_weight(x.T * s[:, None], "e4m3")
    w1_words, w1_scales = pack4(w1 / s[:, None])
    return {
        "x_words": x_words,
        "x_scales": x_scales,
        "w1_words": w1_words,
        "w1_scales": w1_scales,
        "hidden_gain": bf(np.exp(0.3 * np.random.randn(F)) * t),
        "w2": bf(w2 / t[:, None]),
        "proj_bias": bf(0.3 * np.random.randn(D)),
        "dim_weight": bf(np.exp(0.8 * np.random.randn(D))),
        "query_weight": bf(np.exp(0.3 * np.random.randn(Q))),
    }


def reference(x_words, x_scales, w1_words, w1_scales, hidden_gain, w2, proj_bias, dim_weight, query_weight):
    XT = unpack_weight(x_words, x_scales, "e4m3")
    W1 = unpack4(w1_words, w1_scales)
    A = XT.T @ W1
    H = np.tanh(A) * f64(hidden_gain)
    Z = mxq(H, 1, "e4m3") @ mxq(f64(w2), 0, "e4m3")
    y = (Z + f64(proj_bias)) * f64(dim_weight) * f64(query_weight)[:, None]
    words, scales = planes(y.T)
    return y, words, scales

@@ -1,0 +1,294 @@
+from contextlib import ExitStack
+
+import concourse.mybir as mybir
+from concourse.masks import make_identity
+
+Q, E, F, D = 512, 1536, 2048, 1024
+FLOPS = 2 * Q * E * F + 2 * Q * F * D
+
+F32 = mybir.dt.float32
+BF16 = mybir.dt.bfloat16
+I32 = mybir.dt.int32
+U8 = mybir.dt.uint8
+FP8X4 = mybir.dt.float8_e4m3fn_x4
+FP4X4 = mybir.dt.float4_e2m1fn_x4
+ACT = mybir.ActivationFunctionType
+ALU = mybir.AluOpType
+P = 128
+
+ORDER = """ms xsG gain qw xs0 xs1 s0_0 s0_1 s0_2 s0_3 tab ms2 w1c0 x0 w2_00 w2_10 w1c1 s1 w2_20 w1c2 w2_30 w1c3 bd w2_01 qwb w2_11 w2_21 w2_31
+ps0 pw0 s1_00 s1_01 s1_02 s1_03 il000 il001 sc trs il100 il101 pw1 qw00 qw10 ps1 so th00 th01 th02 th03 s1_10 s1_11 s1_12 s1_13 il200 pw2 tt00 tt01
+th10 th11 th12 th13 s1_20 s1_21 s1_22 s1_23 il201 il300 qh0 pw3 tt10 tt11 qw20 th20 th21 th22 th23 s1_30 s1_31 s1_32 s1_33 il301 tt20 tt21 qh1 qh2
+th30 th31 th32 th33 tt30 tt31 qw30 qh3 s2_00 s2_01 s2_02 s2_030 s2_031 s2_032 s2_033 bdc il010 il011 il110 il111 qw01 il210 qw11 il211 il310 u00 u01 u02 u03 il311 qw21 yb00 qw31 yb01
+s2_10 s2_11 tr00 tr01 tr02 s2_12 s2_130 s2_131 s2_132 s2_133 tr03 yo00 st00 yo01 st01 yo02 st02 u100 u110 u120 u130 qy00 qy01 sw0 ss0 u101 u111 u121 u131 yo03 st03
+tr10 tr11 tr12 tr13 yb10 yb11 yo10 st10 yo11 st11 yo12 st12 qy10 qy11 yo13 st13 sw1 ss1""".split()
+ON_SCALAR = """il000 il100 il201 il301 il010 il011 il110 il111 il311 u00 u01 u02 u03 yo00 yo01 yo02 u100 u110 u130 u101 u111 u121 yo10 yo11 yo12 yo13""".split()
+
+
+def tile_tanh_query_tower_h2_kernel(
+    tc, x_words, x_scales, w1_words, w1_scales, hidden_gain, w2, proj_bias, dim_weight, query_weight, out_0, out_1, out_2
+):
+    nc = tc.nc
+    with ExitStack() as ctx:
+        sb = ctx.enter_context(tc.tile_pool(name="sb", bufs=1))
+        ps = ctx.enter_context(tc.psum_pool(name="ps", bufs=1))
+
+        def keep(name, shape, dtype):
+            return sb.tile(shape, dtype, name=name, align_bytes=64)
+
+        x_codes = keep("x_codes", [P, 3, Q], I32)
+        first_planes = keep("first_planes", [P, 2, 3, 512], U8)
+        x_plane = first_planes[:, 0]
+        s_raw0 = first_planes[:, 1]
+        s_raw1 = keep("s_raw1", [P, 3, 1536], U8)
+        s_perm0 = keep("s_perm0", [P, 4, 3, 128], U8)
+        s_perm1 = keep("s_perm1", [P, 4, 3, 3, 128], U8)
+        w1_raw = [keep("w1_raw%d" % g, [P, 3, 256], I32) for g in range(4)]
+        w1_perm = [keep("w1_perm%d" % g, [P, 4, 3, 256], U8) for g in range(4)]
+        ident = keep("ident", [P, P], F32)
+        vec_rows = keep("vec_rows", [P, 512], BF16)
+        vec_f32 = keep("vec_f32", [P, 4, P], F32)
+        gain_t = keep("gain_t", [P, 4, 4], F32)
+        qw_col = keep("qw_col", [P, 4], F32)
+        bd_raw = keep("bd_raw", [P, 2, 16], BF16)
+        dw_col = keep("dw_col", [P, 8], F32)
+        bdw_col = keep("bdw_col", [P, 8], F32)
+        qw_all = keep("qw_all", [P, Q], BF16)
+        warm = keep("warm", [P, 8], F32)
+        tanh_t = [keep("tanh%d" % g, [P, 4, Q], F32) for g in range(3)]
+        tanh_t.append(tanh_t[0])
+        h_bf = 2 * [keep("h_bf%d" % g, [P, Q, 4], BF16) for g in range(2)]
+        h_codes = keep("h_codes", [P, 4, Q], I32)
+        h_plane = keep("h_plane", [P, 4, Q], U8)
+        w2_raw = {(g, h): keep("w2_raw%d%d" % (g, h), [P, 4, 512], BF16) for g in range(4) for h in range(2)}
+        w2_bf = {(g, h): keep("w2_bf%d%d" % (g, h), [P, 4, P, 4], BF16) for g in range(4) for h in range(2)}
+        w2_codes = keep("w2_codes", [P, 4, 2, 512], I32)
+        w2_plane = keep("w2_plane", [P, 4, 2, 512], U8)
+        u_t = [keep("u%d" % h, [P, 4, Q], F32) for h in range(2)]
+        y_rows = {(h, c): keep("y_rows%d%d" % (h, c), [P, 512], F32) for h in range(2) for c in range(4)}
+        y_bf = [keep("y_bf%d" % h, [P, Q, 4], BF16) for h in range(2)]
+        y_codes = [keep("y_codes%d" % h, [P, Q], I32) for h in range(2)]
+        y_plane = [keep("y_plane%d" % h, [P, Q], U8) for h in range(2)]
+        banks = {}
+
+        def bank(index, key):
+            banks[key] = ps.tile([P, 4, P], F32, name="bank%d" % index, tag="bank%d" % index)
+            return banks[key]
+
+        def flat(t):
+            return t[:].rearrange("p a b -> p (a b)")
+
+        def rows_to_plane(queue, plane, rows, quad):
+            queue.dma_start(
+                out=plane[32 * quad : 32 * quad + 4].bitcast(I32),
+                in_=rows[:, 4 * quad : 4 * quad + 4, :].rearrange("e r n -> r e n").bitcast(I32),
+            )
+
+        def first_pass(g, t, e):
+            acc = bank(t, ("a", g, t)) if e == 0 else banks[("a", g, t)]
+            plane = s_perm0[:, t, e, :] if g == 0 else s_perm1[:, t, e, g - 1, :]
+            nc.tensor.matmul_mx(
+                out=flat(acc),
+                lhsT=w1_perm[g][:, t, e, :].bitcast(FP4X4),
+                lhsT_scale=plane,
+                rhs=x_codes[:, e, :].bitcast(FP8X4),
+                rhs_scale=x_plane[:, e, :],
+                start=(e == 0),
+                stop=(e == 2),
+            )
+
+        def second_pass(h, g, t):
+            acc = bank(4 * (1 - h) + t, ("z", h, t)) if g == 0 else banks[("z", h, t)]
+            cols = slice(P * t, P * (t + 1))
+            nc.tensor.matmul_mx(
+                out=flat(acc),
+                lhsT=w2_codes[:, g, h, cols].bitcast(FP8X4),
+                lhsT_scale=w2_plane[:, g, h, cols],
+                rhs=h_codes[:, g, :].bitcast(FP8X4),
+                rhs_scale=h_plane[:, g, :],
+                start=(g == 0),
+                stop=(g == 3),
+            )
+
+        def quantize(codes, plane, src):
+            nc.vector.quantize_mx(out=codes.bitcast(FP8X4), scales=plane, in_=src)
+
+        def step(name):
+            on_act = name in ON_SCALAR
+            d = [int(ch) for ch in name.split("_")[-1] if ch in "0123456789"]
+            if name == "ms":
+                nc.vector.memset(first_planes[:].rearrange("p a e n -> p (a e n)").bitcast(I32), 0)
+            elif name == "ms2":
+                nc.vector.memset(flat(s_raw1).bitcast(I32), 0)
+                nc.vector.memset(flat(vec_f32), 0.0)
+            elif name == "xsG":
+                make_identity(nc, ident[:])
+                rows_to_plane(nc.gpsimd, x_plane, x_scales, 2)
+                rows_to_plane(nc.gpsimd, x_plane, x_scales, 3)
+            elif name == "gain":
+                nc.gpsimd.dma_start(out=vec_rows[0:4, :], in_=hidden_gain.rearrange("(g n) -> g n", g=4))
+            elif name == "qw":
+                nc.gpsimd.dma_start(out=vec_rows[32:33, :], in_=query_weight.rearrange("(g n) -> g n", g=1))
+            elif name.startswith("xs"):
+                rows_to_plane(nc.scalar, x_plane, x_scales, d[0])
+            elif name.startswith("s0_"):
+                rows_to_plane(nc.scalar, s_raw0, w1_scales[:, :, 0:512], d[0])
+            elif name == "s1":
+                for quad in range(4):
+                    rows_to_plane(nc.sync, s_raw1, w1_scales[:, :, 512:2048], quad)
+            elif name == "tab":
+                nc.vector.memset(warm[:], 0.0)
+                nc.scalar.activation(out=warm[:, 4:8], in_=warm[:, 0:4], func=ACT.Tanh)
+            elif name.startswith("w1c"):
+                g = d[-1]
+                nc.sync.dma_start(
+                    out=w1_raw[g][:],
+                    in_=w1_words[:, :, 1024 * g : 1024 * (g + 1)].rearrange("e p n -> p e n").bitcast(I32),
+                )
+            elif name == "x0":
+                es = slice(0, 3)
+                nc.sync.dma_start(
+                    out=x_codes[:, es, :], in_=x_words[es].rearrange("e p n t -> p e (n t)").bitcast(I32)
+                )
+            elif name.startswith("w2_"):
+                g, h = d
+                src = w2[512 * g : 512 * (g + 1), 512 * h : 512 * (h + 1)].rearrange("(i j b) n -> b i j n", j=4, b=4)
+                for b in range(4):
+                    nc.sync.dma_start(out=w2_raw[g, h][b:P:4], in_=src[b])
+            elif name == "qwb":
+                nc.sync.dma_start(out=qw_all[:], in_=query_weight.partition_broadcast(P))
+            elif name == "bd":
+                for j, vec in enumerate((proj_bias, dim_weight)):
+                    nc.sync.dma_start(
+                        out=bd_raw[:, j, 0:8].rearrange("p (h t) -> p h t", t=4),
+                        in_=vec.rearrange("(h p t) -> p h t", p=P, t=4),
+                    )
+            elif name == "bdc":
+                nc.vector.tensor_copy(out=dw_col[:], in_=bd_raw[:, 1, 0:8])
+                nc.vector.tensor_tensor(out=bdw_col[:], in0=bd_raw[:, 0, 0:8], in1=bd_raw[:, 1, 0:8], op=ALU.mult)
+            elif name == "ps0":
+                nc.vector.tensor_copy(
+                    out=s_perm0[:].rearrange("p t e n -> p t (e n)").bitcast(I32).rearrange("p t n -> p n t"),
+                    in_=s_raw0.rearrange("p e n -> p (e n)").bitcast(I32).rearrange("p (n t) -> p n t", t=4),
+                )
+            elif name == "ps1":
+                nc.vector.tensor_copy(
+                    out=s_perm1[:].rearrange("p t e g n -> p t (e g n)").bitcast(I32).rearrange("p t n -> p n t"),
+                    in_=flat(s_raw1).bitcast(I32).rearrange("p (n t) -> p n t", t=4),
+                )
+            elif name.startswith("pw"):
+                g = d[0]
+                nc.vector.tensor_copy(
+                    out=w1_perm[g][:].bitcast(I32).rearrange("p t e (i b) -> p t e i b", b=2),
+                    in_=w1_raw[g][:].rearrange("p e (i t b) -> p t e i b", t=4, b=2),
+                )
+            elif name == "sc":
+                nc.vector.tensor_copy(
+                    out=vec_f32[0:4].rearrange("p t (i b) -> p t i b", b=4),
+                    in_=vec_rows[0:4, :].rearrange("p (i t b) -> p t i b", t=4, b=4),
+                )
+                nc.vector.tensor_copy(out=flat(vec_f32)[32:33, :], in_=vec_rows[32:33, :])
+            elif name == "trs":
+                turned = bank(7, "vec")
+                for t in range(4):
+                    nc.tensor.transpose(turned[:, t, :], vec_f32[:, t, :], ident[:])
+            elif name == "so":
+                turned = banks["vec"]
+                nc.vector.tensor_copy(out=gain_t[:], in_=turned[:, :, 0:4].rearrange("p t g -> p g t"))
+                nc.vector.tensor_copy(out=qw_col[:], in_=turned[:, :, 32])
+            elif name.startswith("s1_0e"):
+                for t in range(4):
+                    first_pass(0, t, d[1])
+            elif name.startswith("s1_"):
+                for e in range(3):
+                    first_pass(d[0], d[1], e)
+            elif name.startswith("th"):
+                g, t = d
+                nc.scalar.activation(out=tanh_t[g][:, t, :], in_=flat(banks[("a", g, t)]), func=ACT.Tanh)
+            elif name.startswith("tt"):
+                g, part = d
+                qs = slice(256 * part, 256 * (part + 1))
+                nc.vector.tensor_tensor(
+                    out=h_bf[g][:, qs, :].rearrange("p (c i) t -> p c t i", i=4),
+                    in0=tanh_t[g][:, :, qs].rearrange("p t (c i) -> p c t i", i=4),
+                    in1=gain_t[:, g, :].unsqueeze(1).unsqueeze(3).to_broadcast([P, 64, 4, 4]),
+                    op=ALU.mult,
+                )
+            elif name.startswith("qh"):
+                g = d[0]
+                quantize(h_codes[:, g, :], h_plane[:, g, :], flat(h_bf[g]))
+            elif name.startswith("il"):
+                g, h, part = d
+                dst = w2_bf[g, h][:, :, 64 * part : 64 * (part + 1), :].rearrange("p t (a e) j -> p a j e t", e=2)
+                src = w2_raw[g, h][:, :, 256 * part : 256 * (part + 1)].rearrange("p j (a e t) -> p a j e t", e=2, t=4)
+                if on_act:
+                    nc.scalar.copy(out=dst, in_=src)
+                else:
+                    nc.vector.tensor_copy(out=dst, in_=src)
+            elif name.startswith("qw") and len(d) == 2:
+                g, h = d
+                quantize(w2_codes[:, g, h, :], w2_plane[:, g, h, :], w2_bf[g, h][:].rearrange("p t m j -> p (t m j)"))
+            elif name.startswith("s2_"):
+                for t in range(4) if len(d) == 2 else d[2:]:
+                    second_pass(d[0], d[1], t)
+            elif name.startswith("u"):
+                h, t = d[:2]
+                qs = slice(0, Q) if len(d) == 2 else slice(256 * d[2], 256 * (d[2] + 1))
+                col = slice(4 * h + t, 4 * h + t + 1)
+                acc = flat(banks[("z", h, t)])[:, qs]
+                if on_act:
+                    nc.scalar.activation(
+                        out=u_t[h][:, t, qs], in_=acc, func=ACT.Identity, scale=dw_col[:, col], bias=bdw_col[:, col]
+                    )
+                else:
+                    nc.vector.tensor_scalar(
+                        out=u_t[h][:, t, qs], in0=acc, scalar1=dw_col[:, col], scalar2=bdw_col[:, col],
+                        op0=ALU.mult, op1=ALU.add,
+                    )
+            elif name.startswith("tr"):
+                h, c = d
+                turned = bank(4 + c, ("y", h, c))
+                for t in range(4):
+                    nc.tensor.transpose(turned[:, t, :], u_t[h][:, t, P * c : P * (c + 1)], ident[:])
+            elif name.startswith("yo"):
+                h, c = d
+                dst = y_rows[h, c][:].rearrange("p (m t) -> p m t", t=4)
+                src = banks[("y", h, c)][:].rearrange("p t m -> p m t")
+                if on_act:
+                    nc.scalar.activation(out=dst, in_=src, func=ACT.Copy, scale=qw_col[:, c : c + 1])
+                else:
+                    nc.vector.tensor_scalar(
+                        out=dst, in0=src, scalar1=qw_col[:, c : c + 1], scalar2=None, op0=ALU.mult
+                    )
+            elif name.startswith("st"):
+                h, c = d
+                nc.sync.dma_start(out=out_0[P * c : P * (c + 1), 512 * h : 512 * (h + 1)], in_=y_rows[h, c][:])
+            elif name.startswith("yb"):
+                h, part = d
+                qs = slice(256 * part, 256 * (part + 1))
+                nc.vector.tensor_tensor(
+                    out=y_bf[h][:, qs, :].rearrange("p (c i) t -> p c t i", i=4),
+                    in0=u_t[h][:, :, qs].rearrange("p t (c i) -> p c t i", i=4),
+                    in1=qw_all[:, qs].rearrange("p (c i) -> p c i", i=4).unsqueeze(2).to_broadcast([P, 64, 4, 4]),
+                    op=ALU.mult,
+                )
+            elif name.startswith("qy"):
+                h, part = d
+                qs = slice(256 * part, 256 * (part + 1))
+                quantize(y_codes[h][:, qs], y_plane[h][:, qs], y_bf[h][:, qs, :].rearrange("p q t -> p (q t)"))
+            elif name.startswith("sw"):
+                h = d[0]
+                nc.sync.dma_start(out=out_1[h].rearrange("p m t -> p (m t)").bitcast(I32), in_=y_codes[h][:])
+            elif name.startswith("ss"):
+                h = d[0]
+                for quad in range(4):
+                    nc.sync.dma_start(
+                        out=out_2[h, 4 * quad : 4 * quad + 4, :].bitcast(I32),
+                        in_=y_plane[h][32 * quad : 32 * quad + 4, :].bitcast(I32),
+                    )
+            else:
+                raise ValueError(name)
+
+        with tc.manual_schedule():
+            for name in ORDER:
+                step(name)

@@ -16,13 +16,13 @@ ACT = mybir.ActivationFunctionType
 ALU = mybir.AluOpType
 P = 128
 
-ORDER = """ms xsG gain qw xs0 xs1 s0_0 s0_1 s0_2 s0_3 tab ms2 w1c0 x0 w2_00 w2_10 w1c1 s1 w2_20 w1c2 w2_30 w1c3 bd w2_01 qwb w2_11 w2_21 w2_31
-ps0 pw0 s1_00 s1_01 s1_02 s1_03 il000 il001 sc trs il100 il101 pw1 qw00 qw10 ps1 so th00 th01 th02 th03 s1_10 s1_11 s1_12 s1_13 il200 pw2 tt00 tt01
-th10 th11 th12 th13 s1_20 s1_21 s1_22 s1_23 il201 il300 qh0 pw3 tt10 tt11 qw20 th20 th21 th22 th23 s1_30 s1_31 s1_32 s1_33 il301 tt20 tt21 qh1 qh2
-th30 th31 th32 th33 tt30 tt31 qw30 qh3 s2_00 s2_01 s2_02 s2_030 s2_031 s2_032 s2_033 bdc il010 il011 il110 il111 qw01 il210 qw11 il211 il310 u00 u01 u02 u03 il311 qw21 yb00 qw31 yb01
-s2_10 s2_11 tr00 tr01 tr02 s2_12 s2_130 s2_131 s2_132 s2_133 tr03 yo00 st00 yo01 st01 yo02 st02 u100 u110 u120 u130 qy00 qy01 sw0 ss0 u101 u111 u121 u131 yo03 st03
-tr10 tr11 tr12 tr13 yb10 yb11 yo10 st10 yo11 st11 yo12 st12 qy10 qy11 yo13 st13 sw1 ss1""".split()
-ON_SCALAR = """il000 il100 il201 il301 il010 il011 il110 il111 il311 u00 u01 u02 u03 yo00 yo01 yo02 u100 u110 u130 u101 u111 u121 yo10 yo11 yo12 yo13""".split()
+ORDER = """ms xsG gain qw xs0 xs1 s0_0 s0_1 s0_2 s0_3 tab w1c0 x0 w2_00 w2_10 ps0 pw0 ms2 s1 w1c1 w2_20 w1c2 w1c3 w2_30 w2_01 w2_11 bd w2_21 w2_31 qwb
+s1_00 s1_01 s1_02 s1_03 il000 il001 sc trs th00 il101 qw00 il100 ps1 pw1 so qw10 th01 th02 th03 s1_10 s1_11 s1_12 s1_13 il201 tt00 pw2 tt01 il200 pw3 qh0
+th10 th11 th12 th13 s1_20 s1_21 s1_22 s1_23 il301 tt10 tt11 qw20 qh1 th20 th21 th22 th23 s1_30 s1_31 s1_32 s1_33 il010 tt20 tt21 il300
+th30 th31 th32 th33 tt30 qh2 tt31 qw30 bdc qh3 s2_00 s2_01 s2_02 s2_030 s2_031 s2_032 s2_033 il011 il110 il111 il210 qw01 il211 qw11 il311 u00 u01 u02 u03 il310 qw21 yb00 qw31 yb01
+s2_10 s2_11 tr00 tr01 tr02 s2_12 s2_130 s2_131 s2_132 s2_133 tr03 yo00 st00 yo01 st01 yo02 st02 qy00 qy01 sw0 ss0 u100 u110 u120 u130 u101 u111 u121 u131 yo03 st03
+tr10 tr11 tr12 tr13 yb10 yb11 yo10 st10 yo11 st11 yo12 st12 qy10 sw10 yo13 st13 qy11 sw11 ss1""".split()
+ON_SCALAR = """il101 il201 il301 il010 il011 il110 il111 il210 il310 u00 u01 u02 yo00 yo01 yo02 u100 u110 u120 u130 u101 u111 yo10 yo11 yo12 yo13""".split()
 
 
 def tile_tanh_query_tower_h2_kernel(
@@ -122,9 +122,9 @@ def tile_tanh_query_tower_h2_kernel(
                 nc.vector.memset(flat(s_raw1).bitcast(I32), 0)
                 nc.vector.memset(flat(vec_f32), 0.0)
             elif name == "xsG":
-                make_identity(nc, ident[:])
                 rows_to_plane(nc.gpsimd, x_plane, x_scales, 2)
                 rows_to_plane(nc.gpsimd, x_plane, x_scales, 3)
+                make_identity(nc, ident[:])
             elif name == "gain":
                 nc.gpsimd.dma_start(out=vec_rows[0:4, :], in_=hidden_gain.rearrange("(g n) -> g n", g=4))
             elif name == "qw":
@@ -168,13 +168,13 @@ def tile_tanh_query_tower_h2_kernel(
                 nc.vector.tensor_tensor(out=bdw_col[:], in0=bd_raw[:, 0, 0:8], in1=bd_raw[:, 1, 0:8], op=ALU.mult)
             elif name == "ps0":
                 nc.vector.tensor_copy(
-                    out=s_perm0[:].rearrange("p t e n -> p t (e n)").bitcast(I32).rearrange("p t n -> p n t"),
-                    in_=s_raw0.rearrange("p e n -> p (e n)").bitcast(I32).rearrange("p (n t) -> p n t", t=4),
+                    out=s_perm0[:].rearrange("p t e n -> p t (e n)").bitcast(I32).rearrange("p t (a i) -> p a t i", i=4),
+                    in_=s_raw0.rearrange("p e n -> p (e n)").bitcast(I32).rearrange("p (a i t) -> p a t i", i=4, t=4),
                 )
             elif name == "ps1":
                 nc.vector.tensor_copy(
-                    out=s_perm1[:].rearrange("p t e g n -> p t (e g n)").bitcast(I32).rearrange("p t n -> p n t"),
-                    in_=flat(s_raw1).bitcast(I32).rearrange("p (n t) -> p n t", t=4),
+                    out=s_perm1[:].rearrange("p t e g n -> p t (e g n)").bitcast(I32).rearrange("p t (a i) -> p a t i", i=4),
+                    in_=flat(s_raw1).bitcast(I32).rearrange("p (a i t) -> p a t i", i=4, t=4),
                 )
             elif name.startswith("pw"):
                 g = d[0]
@@ -209,9 +209,9 @@ def tile_tanh_query_tower_h2_kernel(
                 g, part = d
                 qs = slice(256 * part, 256 * (part + 1))
                 nc.vector.tensor_tensor(
-                    out=h_bf[g][:, qs, :].rearrange("p (c i) t -> p c t i", i=4),
-                    in0=tanh_t[g][:, :, qs].rearrange("p t (c i) -> p c t i", i=4),
-                    in1=gain_t[:, g, :].unsqueeze(1).unsqueeze(3).to_broadcast([P, 64, 4, 4]),
+                    out=h_bf[g][:, qs, :].rearrange("p (c i) t -> p c t i", i=2),
+                    in0=tanh_t[g][:, :, qs].rearrange("p t (c i) -> p c t i", i=2),
+                    in1=gain_t[:, g, :].unsqueeze(1).unsqueeze(3).to_broadcast([P, 128, 4, 2]),
                     op=ALU.mult,
                 )
             elif name.startswith("qh"):
@@ -219,8 +219,8 @@ def tile_tanh_query_tower_h2_kernel(
                 quantize(h_codes[:, g, :], h_plane[:, g, :], flat(h_bf[g]))
             elif name.startswith("il"):
                 g, h, part = d
-                dst = w2_bf[g, h][:, :, 64 * part : 64 * (part + 1), :].rearrange("p t (a e) j -> p a j e t", e=2)
-                src = w2_raw[g, h][:, :, 256 * part : 256 * (part + 1)].rearrange("p j (a e t) -> p a j e t", e=2, t=4)
+                dst = w2_bf[g, h][:, :, 64 * part : 64 * (part + 1), :].rearrange("p t (a e) j -> p a t e j", e=2)
+                src = w2_raw[g, h][:, :, 256 * part : 256 * (part + 1)].rearrange("p j (a e t) -> p a t e j", e=2, t=4)
                 if on_act:
                     nc.scalar.copy(out=dst, in_=src)
                 else:
@@ -267,9 +267,9 @@ def tile_tanh_query_tower_h2_kernel(
                 h, part = d
                 qs = slice(256 * part, 256 * (part + 1))
                 nc.vector.tensor_tensor(
-                    out=y_bf[h][:, qs, :].rearrange("p (c i) t -> p c t i", i=4),
-                    in0=u_t[h][:, :, qs].rearrange("p t (c i) -> p c t i", i=4),
-                    in1=qw_all[:, qs].rearrange("p (c i) -> p c i", i=4).unsqueeze(2).to_broadcast([P, 64, 4, 4]),
+                    out=y_bf[h][:, qs, :].rearrange("p (c i) t -> p c t i", i=2),
+                    in0=u_t[h][:, :, qs].rearrange("p t (c i) -> p c t i", i=2),
+                    in1=qw_all[:, qs].rearrange("p (c i) -> p c i", i=2).unsqueeze(2).to_broadcast([P, 128, 4, 2]),
                     op=ALU.mult,
                 )
             elif name.startswith("qy"):
@@ -278,7 +278,8 @@ def tile_tanh_query_tower_h2_kernel(
                 quantize(y_codes[h][:, qs], y_plane[h][:, qs], y_bf[h][:, qs, :].rearrange("p q t -> p (q t)"))
             elif name.startswith("sw"):
                 h = d[0]
-                nc.sync.dma_start(out=out_1[h].rearrange("p m t -> p (m t)").bitcast(I32), in_=y_codes[h][:])
+                qs = slice(0, Q) if len(d) == 1 else slice(256 * d[1], 256 * (d[1] + 1))
+                nc.sync.dma_start(out=out_1[h].rearrange("p m t -> p (m t)").bitcast(I32)[:, qs], in_=y_codes[h][:, qs])
             elif name.startswith("ss"):
                 h = d[0]
                 for quad in range(4):

from contextlib import ExitStack

import concourse.mybir as mybir
from concourse.masks import make_identity

Q, E, F, D = 512, 1536, 2048, 1024
FLOPS = 2 * Q * E * F + 2 * Q * F * D

F32 = mybir.dt.float32
BF16 = mybir.dt.bfloat16
I32 = mybir.dt.int32
U8 = mybir.dt.uint8
FP8X4 = mybir.dt.float8_e4m3fn_x4
FP4X4 = mybir.dt.float4_e2m1fn_x4
ACT = mybir.ActivationFunctionType
ALU = mybir.AluOpType
P = 128

ORDER = """ms xsG gain qw xs0 xs1 s0_0 s0_1 s0_2 s0_3 tab w1c0 x0 w2_00 w2_10 ps0 pw0 ms2 s1 w1c1 w2_20 w1c2 w1c3 w2_30 w2_01 w2_11 bd w2_21 w2_31 qwb
s1_00 s1_01 s1_02 s1_03 il000 il001 sc trs th00 il101 qw00 il100 ps1 pw1 so qw10 th01 th02 th03 s1_10 s1_11 s1_12 s1_13 il201 tt00 pw2 tt01 il200 pw3 qh0
th10 th11 th12 th13 s1_20 s1_21 s1_22 s1_23 il301 tt10 tt11 qw20 qh1 th20 th21 th22 th23 s1_30 s1_31 s1_32 s1_33 il010 tt20 tt21 il300
th30 th31 th32 th33 tt30 qh2 tt31 qw30 bdc qh3 s2_00 s2_01 s2_02 s2_030 s2_031 s2_032 s2_033 il011 il110 il111 il210 qw01 il211 qw11 il311 u00 u01 u02 u03 il310 qw21 yb00 qw31 yb01
s2_10 s2_11 tr00 tr01 tr02 s2_12 s2_130 s2_131 s2_132 s2_133 tr03 yo00 st00 yo01 st01 yo02 st02 qy00 qy01 sw0 ss0 u100 u110 u120 u130 u101 u111 u121 u131 yo03 st03
tr10 tr11 tr12 tr13 yb10 yb11 yo10 st10 yo11 st11 yo12 st12 qy10 sw10 yo13 st13 qy11 sw11 ss1""".split()
ON_SCALAR = """il101 il201 il301 il010 il011 il110 il111 il210 il310 u00 u01 u02 yo00 yo01 yo02 u100 u110 u120 u130 u101 u111 yo10 yo11 yo12 yo13""".split()


def tile_tanh_query_tower_h2_kernel(
    tc, x_words, x_scales, w1_words, w1_scales, hidden_gain, w2, proj_bias, dim_weight, query_weight, out_0, out_1, out_2
):
    nc = tc.nc
    with ExitStack() as ctx:
        sb = ctx.enter_context(tc.tile_pool(name="sb", bufs=1))
        ps = ctx.enter_context(tc.psum_pool(name="ps", bufs=1))

        def keep(name, shape, dtype):
            return sb.tile(shape, dtype, name=name, align_bytes=64)

        x_codes = keep("x_codes", [P, 3, Q], I32)
        first_planes = keep("first_planes", [P, 2, 3, 512], U8)
        x_plane = first_planes[:, 0]
        s_raw0 = first_planes[:, 1]
        s_raw1 = keep("s_raw1", [P, 3, 1536], U8)
        s_perm0 = keep("s_perm0", [P, 4, 3, 128], U8)
        s_perm1 = keep("s_perm1", [P, 4, 3, 3, 128], U8)
        w1_raw = [keep("w1_raw%d" % g, [P, 3, 256], I32) for g in range(4)]
        w1_perm = [keep("w1_perm%d" % g, [P, 4, 3, 256], U8) for g in range(4)]
        ident = keep("ident", [P, P], F32)
        vec_rows = keep("vec_rows", [P, 512], BF16)
        vec_f32 = keep("vec_f32", [P, 4, P], F32)
        gain_t = keep("gain_t", [P, 4, 4], F32)
        qw_col = keep("qw_col", [P, 4], F32)
        bd_raw = keep("bd_raw", [P, 2, 16], BF16)
        dw_col = keep("dw_col", [P, 8], F32)
        bdw_col = keep("bdw_col", [P, 8], F32)
        qw_all = keep("qw_all", [P, Q], BF16)
        warm = keep("warm", [P, 8], F32)
        tanh_t = [keep("tanh%d" % g, [P, 4, Q], F32) for g in range(3)]
        tanh_t.append(tanh_t[0])
        h_bf = 2 * [keep("h_bf%d" % g, [P, Q, 4], BF16) for g in range(2)]
        h_codes = keep("h_codes", [P, 4, Q], I32)
        h_plane = keep("h_plane", [P, 4, Q], U8)
        w2_raw = {(g, h): keep("w2_raw%d%d" % (g, h), [P, 4, 512], BF16) for g in range(4) for h in range(2)}
        w2_bf = {(g, h): keep("w2_bf%d%d" % (g, h), [P, 4, P, 4], BF16) for g in range(4) for h in range(2)}
        w2_codes = keep("w2_codes", [P, 4, 2, 512], I32)
        w2_plane = keep("w2_plane", [P, 4, 2, 512], U8)
        u_t = [keep("u%d" % h, [P, 4, Q], F32) for h in range(2)]
        y_rows = {(h, c): keep("y_rows%d%d" % (h, c), [P, 512], F32) for h in range(2) for c in range(4)}
        y_bf = [keep("y_bf%d" % h, [P, Q, 4], BF16) for h in range(2)]
        y_codes = [keep("y_codes%d" % h, [P, Q], I32) for h in range(2)]
        y_plane = [keep("y_plane%d" % h, [P, Q], U8) for h in range(2)]
        banks = {}

        def bank(index, key):
            banks[key] = ps.tile([P, 4, P], F32, name="bank%d" % index, tag="bank%d" % index)
            return banks[key]

        def flat(t):
            return t[:].rearrange("p a b -> p (a b)")

        def rows_to_plane(queue, plane, rows, quad):
            queue.dma_start(
                out=plane[32 * quad : 32 * quad + 4].bitcast(I32),
                in_=rows[:, 4 * quad : 4 * quad + 4, :].rearrange("e r n -> r e n").bitcast(I32),
            )

        def first_pass(g, t, e):
            acc = bank(t, ("a", g, t)) if e == 0 else banks[("a", g, t)]
            plane = s_perm0[:, t, e, :] if g == 0 else s_perm1[:, t, e, g - 1, :]
            nc.tensor.matmul_mx(
                out=flat(acc),
                lhsT=w1_perm[g][:, t, e, :].bitcast(FP4X4),
                lhsT_scale=plane,
                rhs=x_codes[:, e, :].bitcast(FP8X4),
                rhs_scale=x_plane[:, e, :],
                start=(e == 0),
                stop=(e == 2),
            )

        def second_pass(h, g, t):
            acc = bank(4 * (1 - h) + t, ("z", h, t)) if g == 0 else banks[("z", h, t)]
            cols = slice(P * t, P * (t + 1))
            nc.tensor.matmul_mx(
                out=flat(acc),
                lhsT=w2_codes[:, g, h, cols].bitcast(FP8X4),
                lhsT_scale=w2_plane[:, g, h, cols],
                rhs=h_codes[:, g, :].bitcast(FP8X4),
                rhs_scale=h_plane[:, g, :],
                start=(g == 0),
                stop=(g == 3),
            )

        def quantize(codes, plane, src):
            nc.vector.quantize_mx(out=codes.bitcast(FP8X4), scales=plane, in_=src)

        def step(name):
            on_act = name in ON_SCALAR
            d = [int(ch) for ch in name.split("_")[-1] if ch in "0123456789"]
            if name == "ms":
                nc.vector.memset(first_planes[:].rearrange("p a e n -> p (a e n)").bitcast(I32), 0)
            elif name == "ms2":
                nc.vector.memset(flat(s_raw1).bitcast(I32), 0)
                nc.vector.memset(flat(vec_f32), 0.0)
            elif name == "xsG":
                rows_to_plane(nc.gpsimd, x_plane, x_scales, 2)
                rows_to_plane(nc.gpsimd, x_plane, x_scales, 3)
                make_identity(nc, ident[:])
            elif name == "gain":
                nc.gpsimd.dma_start(out=vec_rows[0:4, :], in_=hidden_gain.rearrange("(g n) -> g n", g=4))
            elif name == "qw":
                nc.gpsimd.dma_start(out=vec_rows[32:33, :], in_=query_weight.rearrange("(g n) -> g n", g=1))
            elif name.startswith("xs"):
                rows_to_plane(nc.scalar, x_plane, x_scales, d[0])
            elif name.startswith("s0_"):
                rows_to_plane(nc.scalar, s_raw0, w1_scales[:, :, 0:512], d[0])
            elif name == "s1":
                for quad in range(4):
                    rows_to_plane(nc.sync, s_raw1, w1_scales[:, :, 512:2048], quad)
            elif name == "tab":
                nc.vector.memset(warm[:], 0.0)
                nc.scalar.activation(out=warm[:, 4:8], in_=warm[:, 0:4], func=ACT.Tanh)
            elif name.startswith("w1c"):
                g = d[-1]
                nc.sync.dma_start(
                    out=w1_raw[g][:],
                    in_=w1_words[:, :, 1024 * g : 1024 * (g + 1)].rearrange("e p n -> p e n").bitcast(I32),
                )
            elif name == "x0":
                es = slice(0, 3)
                nc.sync.dma_start(
                    out=x_codes[:, es, :], in_=x_words[es].rearrange("e p n t -> p e (n t)").bitcast(I32)
                )
            elif name.startswith("w2_"):
                g, h = d
                src = w2[512 * g : 512 * (g + 1), 512 * h : 512 * (h + 1)].rearrange("(i j b) n -> b i j n", j=4, b=4)
                for b in range(4):
                    nc.sync.dma_start(out=w2_raw[g, h][b:P:4], in_=src[b])
            elif name == "qwb":
                nc.sync.dma_start(out=qw_all[:], in_=query_weight.partition_broadcast(P))
            elif name == "bd":
                for j, vec in enumerate((proj_bias, dim_weight)):
                    nc.sync.dma_start(
                        out=bd_raw[:, j, 0:8].rearrange("p (h t) -> p h t", t=4),
                        in_=vec.rearrange("(h p t) -> p h t", p=P, t=4),
                    )
            elif name == "bdc":
                nc.vector.tensor_copy(out=dw_col[:], in_=bd_raw[:, 1, 0:8])
                nc.vector.tensor_tensor(out=bdw_col[:], in0=bd_raw[:, 0, 0:8], in1=bd_raw[:, 1, 0:8], op=ALU.mult)
            elif name == "ps0":
                nc.vector.tensor_copy(
                    out=s_perm0[:].rearrange("p t e n -> p t (e n)").bitcast(I32).rearrange("p t (a i) -> p a t i", i=4),
                    in_=s_raw0.rearrange("p e n -> p (e n)").bitcast(I32).rearrange("p (a i t) -> p a t i", i=4, t=4),
                )
            elif name == "ps1":
                nc.vector.tensor_copy(
                    out=s_perm1[:].rearrange("p t e g n -> p t (e g n)").bitcast(I32).rearrange("p t (a i) -> p a t i", i=4),
                    in_=flat(s_raw1).bitcast(I32).rearrange("p (a i t) -> p a t i", i=4, t=4),
                )
            elif name.startswith("pw"):
                g = d[0]
                nc.vector.tensor_copy(
                    out=w1_perm[g][:].bitcast(I32).rearrange("p t e (i b) -> p t e i b", b=2),
                    in_=w1_raw[g][:].rearrange("p e (i t b) -> p t e i b", t=4, b=2),
                )
            elif name == "sc":
                nc.vector.tensor_copy(
                    out=vec_f32[0:4].rearrange("p t (i b) -> p t i b", b=4),
                    in_=vec_rows[0:4, :].rearrange("p (i t b) -> p t i b", t=4, b=4),
                )
                nc.vector.tensor_copy(out=flat(vec_f32)[32:33, :], in_=vec_rows[32:33, :])
            elif name == "trs":
                turned = bank(7, "vec")
                for t in range(4):
                    nc.tensor.transpose(turned[:, t, :], vec_f32[:, t, :], ident[:])
            elif name == "so":
                turned = banks["vec"]
                nc.vector.tensor_copy(out=gain_t[:], in_=turned[:, :, 0:4].rearrange("p t g -> p g t"))
                nc.vector.tensor_copy(out=qw_col[:], in_=turned[:, :, 32])
            elif name.startswith("s1_0e"):
                for t in range(4):
                    first_pass(0, t, d[1])
            elif name.startswith("s1_"):
                for e in range(3):
                    first_pass(d[0], d[1], e)
            elif name.startswith("th"):
                g, t = d
                nc.scalar.activation(out=tanh_t[g][:, t, :], in_=flat(banks[("a", g, t)]), func=ACT.Tanh)
            elif name.startswith("tt"):
                g, part = d
                qs = slice(256 * part, 256 * (part + 1))
                nc.vector.tensor_tensor(
                    out=h_bf[g][:, qs, :].rearrange("p (c i) t -> p c t i", i=2),
                    in0=tanh_t[g][:, :, qs].rearrange("p t (c i) -> p c t i", i=2),
                    in1=gain_t[:, g, :].unsqueeze(1).unsqueeze(3).to_broadcast([P, 128, 4, 2]),
                    op=ALU.mult,
                )
            elif name.startswith("qh"):
                g = d[0]
                quantize(h_codes[:, g, :], h_plane[:, g, :], flat(h_bf[g]))
            elif name.startswith("il"):
                g, h, part = d
                dst = w2_bf[g, h][:, :, 64 * part : 64 * (part + 1), :].rearrange("p t (a e) j -> p a t e j", e=2)
                src = w2_raw[g, h][:, :, 256 * part : 256 * (part + 1)].rearrange("p j (a e t) -> p a t e j", e=2, t=4)
                if on_act:
                    nc.scalar.copy(out=dst, in_=src)
                else:
                    nc.vector.tensor_copy(out=dst, in_=src)
            elif name.startswith("qw") and len(d) == 2:
                g, h = d
                quantize(w2_codes[:, g, h, :], w2_plane[:, g, h, :], w2_bf[g, h][:].rearrange("p t m j -> p (t m j)"))
            elif name.startswith("s2_"):
                for t in range(4) if len(d) == 2 else d[2:]:
                    second_pass(d[0], d[1], t)
            elif name.startswith("u"):
                h, t = d[:2]
                qs = slice(0, Q) if len(d) == 2 else slice(256 * d[2], 256 * (d[2] + 1))
                col = slice(4 * h + t, 4 * h + t + 1)
                acc = flat(banks[("z", h, t)])[:, qs]
                if on_act:
                    nc.scalar.activation(
                        out=u_t[h][:, t, qs], in_=acc, func=ACT.Identity, scale=dw_col[:, col], bias=bdw_col[:, col]
                    )
                else:
                    nc.vector.tensor_scalar(
                        out=u_t[h][:, t, qs], in0=acc, scalar1=dw_col[:, col], scalar2=bdw_col[:, col],
                        op0=ALU.mult, op1=ALU.add,
                    )
            elif name.startswith("tr"):
                h, c = d
                turned = bank(4 + c, ("y", h, c))
                for t in range(4):
                    nc.tensor.transpose(turned[:, t, :], u_t[h][:, t, P * c : P * (c + 1)], ident[:])
            elif name.startswith("yo"):
                h, c = d
                dst = y_rows[h, c][:].rearrange("p (m t) -> p m t", t=4)
                src = banks[("y", h, c)][:].rearrange("p t m -> p m t")
                if on_act:
                    nc.scalar.activation(out=dst, in_=src, func=ACT.Copy, scale=qw_col[:, c : c + 1])
                else:
                    nc.vector.tensor_scalar(
                        out=dst, in0=src, scalar1=qw_col[:, c : c + 1], scalar2=None, op0=ALU.mult
                    )
            elif name.startswith("st"):
                h, c = d
                nc.sync.dma_start(out=out_0[P * c : P * (c + 1), 512 * h : 512 * (h + 1)], in_=y_rows[h, c][:])
            elif name.startswith("yb"):
                h, part = d
                qs = slice(256 * part, 256 * (part + 1))
                nc.vector.tensor_tensor(
                    out=y_bf[h][:, qs, :].rearrange("p (c i) t -> p c t i", i=2),
                    in0=u_t[h][:, :, qs].rearrange("p t (c i) -> p c t i", i=2),
                    in1=qw_all[:, qs].rearrange("p (c i) -> p c i", i=2).unsqueeze(2).to_broadcast([P, 128, 4, 2]),
                    op=ALU.mult,
                )
            elif name.startswith("qy"):
                h, part = d
                qs = slice(256 * part, 256 * (part + 1))
                quantize(y_codes[h][:, qs], y_plane[h][:, qs], y_bf[h][:, qs, :].rearrange("p q t -> p (q t)"))
            elif name.startswith("sw"):
                h = d[0]
                qs = slice(0, Q) if len(d) == 1 else slice(256 * d[1], 256 * (d[1] + 1))
                nc.sync.dma_start(out=out_1[h].rearrange("p m t -> p (m t)").bitcast(I32)[:, qs], in_=y_codes[h][:, qs])
            elif name.startswith("ss"):
                h = d[0]
                for quad in range(4):
                    nc.sync.dma_start(
                        out=out_2[h, 4 * quad : 4 * quad + 4, :].bitcast(I32),
                        in_=y_plane[h][32 * quad : 32 * quad + 4, :].bitcast(I32),
                    )
            else:
                raise ValueError(name)

        with tc.manual_schedule():
            for name in ORDER:
                step(name)
